import numpy as np
import ml_dtypes


def mxq(x, axis, fmt="e4m3"):
    dtype, down = {"e4m3": (ml_dtypes.float8_e4m3fn, 7), "e5m2": (ml_dtypes.float8_e5m2, 14)}[fmt]
    v = np.moveaxis(np.asarray(x, np.float32).astype(ml_dtypes.bfloat16).astype(np.float64), axis, -1)
    blocks = v.reshape(v.shape[:-1] + (-1, 32))
    amax = np.abs(blocks).max(-1, keepdims=True)
    byte = np.maximum(np.where(amax > 0, np.frexp(amax)[1] - 1 + 127, 0) - down, 1)
    scale = np.exp2(byte - 127.0)
    codes = (blocks / scale).astype(np.float32).astype(dtype).astype(np.float64)
    return np.moveaxis((codes * scale).reshape(v.shape), -1, axis)


WIDE = False


def mx_kscale(k):
    if not WIDE:
        return np.ones(k)
    levels = np.array([10, -10, 5, -5, 0])
    if k % 512:
        return np.exp2(np.random.permutation(np.resize(levels, k // 32))).repeat(32)
    a = np.empty((k // 512, 16))
    for p in range(k // 512):
        a[p, :8] = np.random.permutation(np.resize(levels, 8))
        for g in range(8):
            far = levels[np.abs(levels - a[p, g]) >= 10]
            a[p, g + 8] = far[np.random.randint(len(far))]
    return np.exp2(a.ravel()).repeat(32)


def f64(x):
    return np.asarray(x).astype(np.float64)


def striped8(idx):
    return np.asarray(idx).reshape(8, -1, 16).transpose(0, 2, 1).reshape(128, -1).astype(np.uint16)


def unstriped8(offs):
    return offs.reshape(8, 16, -1).transpose(0, 2, 1).reshape(8, -1).astype(np.int64)


def pick8(x, idx, run):
    r = np.arange(len(x))
    return x[r[:, None], idx[r % (8 * run) // run]]


E2M1 = np.array([0.0, 0.5, 1.0, 1.5, 2.0, 3.0, 4.0, 6.0, -0.0, -0.5, -1.0, -1.5, -2.0, -3.0, -4.0, -6.0])


def pack_weight(w, fmt):
    k, n = w.shape
    w = f64(np.asarray(w, np.float32).astype(ml_dtypes.bfloat16)).reshape(k // 32, 32, n)
    amax = np.abs(w).max(1)
    if fmt == "e4m3":
        byte = np.frexp(amax)[1] - 1 + 127 - 7
    else:
        mant, ex = np.frexp(amax / 6.0)
        byte = np.where(mant > 0.5, ex, ex - 1) + 127
    byte = np.clip(np.where(amax > 0, byte, 1), 1, 254)
    scaled = (w * np.exp2(127.0 - byte)[:, None, :]).reshape(k, n).astype(np.float32)
    by_word = np.ascontiguousarray(scaled.reshape(k // 512, 128, 4, n).transpose(0, 1, 3, 2))
    if fmt == "e4m3":
        words = by_word.astype(ml_dtypes.float8_e4m3fn).view(np.uint8)
    else:
        c = by_word.astype(ml_dtypes.float4_e2m1fn).view(np.uint8) & 0xF
        words = (c[..., 0::2] | (c[..., 1::2] << 4)).reshape(k // 512, 128, 2 * n)
    return np.ascontiguousarray(words), np.ascontiguousarray(byte.astype(np.uint8).reshape(k // 512, 16, n))


def unpack_weight(words, scales, fmt):
    g, _, n = scales.shape
    words = np.ascontiguousarray(words).reshape(g, 128, n, -1)
    if fmt == "e4m3":
        vals = words.view(ml_dtypes.float8_e4m3fn).astype(np.float64)
    else:
        nib = np.empty((g, 128, n, 4), np.uint8)
        nib[..., 0::2] = words & 0xF
        nib[..., 1::2] = words >> 4
        vals = E2M1[nib]
    vals = vals * np.repeat(np.exp2(scales.astype(np.float64) - 127.0), 8, axis=1)[..., None]
    return vals.transpose(0, 1, 3, 2).reshape(g * 512, n)


D, T, I, Q = 512, 1024, 512, 128


def setup_inputs():
    n = np.random.standard_normal
    idx = np.stack([np.random.permutation(T)[:I] for _ in range(8)])
    idx2 = np.stack([np.random.permutation(T)[:I] for _ in range(8)])
    idx3 = np.stack([np.random.permutation(T)[:I] for _ in range(8)])
    fd = mx_kscale(D)
    keysp = pack_weight(n((D, T)) / fd[:, None], "e4m3")
    return {
        "query": (n((D, Q)) * 1.0 / np.sqrt(D) * fd[:, None]).astype(np.float32),
        "keys_words": keysp[0],
        "keys_scales": keysp[1],
        "old": (1.0 * n((Q, T))).astype(np.float32),
        "offs": striped8(idx),
        "offs2": striped8(idx2),
        "offs3": striped8(idx3),
    }


def reference(query, keys_words, keys_scales, old, offs, offs2, offs3):
    idx = unstriped8(offs)
    idx2 = unstriped8(offs2)
    idx3 = unstriped8(offs3)
    keysu = unpack_weight(keys_words, keys_scales, "e4m3")
    queryq = mxq(f64(query), 0, "e4m3")
    a = queryq.T @ keysu
    w = pick8(a, idx, 16) - pick8(a, idx2, 16)
    f1 = np.zeros((Q, T))
    f1[np.arange(Q)[:, None], idx[np.arange(Q) % 128 // 16]] = w
    f2 = f1 + f64(old)
    y = pick8(f2, idx3, 16) * w
    return y

@@ -1,0 +1,108 @@
+from contextlib import ExitStack
+
+import concourse.mybir as mybir
+
+D, T, I, Q = 512, 1024, 512, 128
+FLOPS = 2 * D * Q * T
+
+F32 = mybir.dt.float32
+BF16 = mybir.dt.bfloat16
+I32 = mybir.dt.int32
+U32 = mybir.dt.uint32
+U16 = mybir.dt.uint16
+U8 = mybir.dt.uint8
+FP8X4 = mybir.dt.float8_e4m3fn_x4
+ADD = mybir.AluOpType.add
+MULT = mybir.AluOpType.mult
+COPY = mybir.ActivationFunctionType.Copy
+
+P = 128
+PACK = 4
+LIST_COLS = I // 16
+KEY_LOAD = 512
+N_MM = 256
+HALF = I // 2
+
+
+def tile_attend_difference_lean_throughtimes_heads_kernel(tc, query, keys_words, keys_scales, old, offs, offs2, offs3, out):
+    nc = tc.nc
+    with ExitStack() as ctx:
+        sb = ctx.enter_context(tc.tile_pool(name="sb", bufs=1))
+        ps = ctx.enter_context(tc.psum_pool(name="ps", bufs=1))
+
+        k_scale = sb.tile([P, T], U8, name="k_scale", align_bytes=64)
+        nc.vector.memset(k_scale[:].bitcast(I32), 0)
+        scale_rows = keys_scales[0].bitcast(I32)
+        for quad in range(4):
+            nc.scalar.dma_start(out=k_scale[32 * quad : 32 * quad + 4, :].bitcast(I32), in_=scale_rows[4 * quad : 4 * quad + 4, :])
+
+        q_raw = sb.tile([P, PACK, Q], F32, name="q_raw")
+        nc.sync.dma_start(out=q_raw[:], in_=query.rearrange("(p j) q -> p j q", j=PACK))
+        words = keys_words[0].rearrange("p n t -> p (n t)").bitcast(I32)
+        k_codes = []
+        for c in range(T // KEY_LOAD):
+            t = sb.tile([P, KEY_LOAD], U32, name="k_codes%d" % c, align_bytes=64)
+            nc.sync.dma_start(out=t[:].bitcast(I32), in_=words[:, c * KEY_LOAD : (c + 1) * KEY_LOAD])
+            k_codes.append(t)
+        list2 = sb.tile([P, LIST_COLS], U16, name="list2")
+        nc.sync.dma_start(list2[:], offs2)
+        list1 = sb.tile([P, LIST_COLS], U16, name="list1")
+        nc.sync.dma_start(list1[:], offs)
+        old_sb = sb.tile([P, T], F32, name="old_sb")
+        nc.sync.dma_start(out=old_sb[:], in_=old)
+        list3 = sb.tile([P, LIST_COLS], U16, name="list3")
+        nc.sync.dma_start(list3[:], offs3)
+
+        f1 = sb.tile([P, T], F32, name="f1")
+        nc.vector.memset(f1[:], 0.0)
+
+        q_bf = sb.tile([P, Q, PACK], BF16, name="q_bf", align_bytes=64)
+        nc.vector.tensor_copy(
+            out=q_bf[:].rearrange("p (c i) j -> p c j i", i=4),
+            in_=q_raw[:].rearrange("p j (c i) -> p c j i", i=4),
+        )
+        q_codes = sb.tile([P, Q], U32, name="q_codes", align_bytes=64)
+        q_scale = sb.tile([P, Q], U8, name="q_scale", align_bytes=64)
+        nc.vector.quantize_mx(out=q_codes[:].bitcast(FP8X4), scales=q_scale[:], in_=q_bf[:].rearrange("p q j -> p (q j)"))
+
+        a = sb.tile([P, T], F32, name="a")
+        for m in range(T // N_MM):
+            t0 = m * N_MM
+            bank = ps.tile([P, N_MM], F32, name="bank%d" % m)
+            codes = k_codes[t0 // KEY_LOAD]
+            c0 = t0 % KEY_LOAD
+            nc.tensor.matmul_mx(
+                out=bank[:],
+                lhsT=q_codes[:].bitcast(FP8X4),
+                lhsT_scale=q_scale[:],
+                rhs=codes[:, c0 : c0 + N_MM].bitcast(FP8X4),
+                rhs_scale=k_scale[:, t0 : t0 + N_MM],
+                start=True,
+                stop=True,
+            )
+            if m % 2 == 0:
+                nc.vector.tensor_copy(out=a[:, t0 : t0 + N_MM], in_=bank[:])
+            else:
+                nc.scalar.activation(a[:, t0 : t0 + N_MM], bank[:], COPY)
+
+        def half(lst, h):
+            return lst[:, h * LIST_COLS // 2 : (h + 1) * LIST_COLS // 2]
+
+        plus = [sb.tile([P, HALF], F32, name="plus%d" % h) for h in range(2)]
+        minus = [sb.tile([P, HALF], F32, name="minus%d" % h) for h in range(2)]
+        w = [sb.tile([P, HALF], F32, name="w%d" % h) for h in range(2)]
+        nc.vector.tensor_scalar(minus[0][:], a[:].indirect(half(list2, 0)), -1.0, 0.0, MULT, ADD)
+        nc.scalar.activation(plus[0][:], a[:].indirect(half(list1, 0)), COPY)
+        nc.scalar.activation(plus[1][:], a[:].indirect(half(list1, 1)), COPY)
+        nc.scalar.activation(minus[1][:], a[:].indirect(half(list2, 1)), COPY, scale=-1.0)
+
+        for h in range(2):
+            nc.vector.tensor_tensor(f1[:].indirect(half(list1, h)), plus[h][:], minus[h][:], ADD)
+            nc.vector.tensor_tensor(w[h][:], plus[h][:], minus[h][:], ADD)
+
+        f2 = sb.tile([P, T], F32, name="f2")
+        nc.vector.tensor_tensor(f2[:], f1[:], old_sb[:], ADD)
+        for h in range(2):
+            y = sb.tile([P, HALF], F32, name="y%d" % h)
+            nc.vector.tensor_tensor(y[:], f2[:].indirect(half(list3, h)), w[h][:], MULT)
+            nc.sync.dma_start(out=out[:, h * HALF : (h + 1) * HALF], in_=y[:])

@@ -22,6 +22,8 @@ LIST_COLS = I // 16
 KEY_LOAD = 512
 N_MM = 256
 HALF = I // 2
+PASSES = ((0, 256), (256, 256), (512, 256), (768, 128), (896, 128))
+PIECES = ((0, 256), (256, 128), (384, 128))
 
 
 def tile_attend_difference_lean_throughtimes_heads_kernel(tc, query, keys_words, keys_scales, old, offs, offs2, offs3, out):
@@ -30,26 +32,27 @@ def tile_attend_difference_lean_throughtimes_heads_kernel(tc, query, keys_words,
         sb = ctx.enter_context(tc.tile_pool(name="sb", bufs=1))
         ps = ctx.enter_context(tc.psum_pool(name="ps", bufs=1))
 
-        k_scale = sb.tile([P, T], U8, name="k_scale", align_bytes=64)
+        q_rows = query.rearrange("(p j) q -> p j q", j=PACK)
+        q_raw = [sb.tile([P, 2, Q], F32, name="q_raw%d" % u, tag="raw%d" % u) for u in range(2)]
+        for u in range(2):
+            nc.sync.dma_start(out=q_raw[u][:], in_=q_rows[:, 2 * u : 2 * u + 2, :])
+        words = keys_words[0].rearrange("p n t -> p (n t)").bitcast(I32)
+        k_codes = [sb.tile([P, KEY_LOAD], U32, name="k_codes%d" % c, align_bytes=64) for c in range(T // KEY_LOAD)]
+        k_scale = sb.tile([P, N_MM], U8, name="k_scale", align_bytes=64)
         nc.vector.memset(k_scale[:].bitcast(I32), 0)
         scale_rows = keys_scales[0].bitcast(I32)
+        nc.sync.dma_start(out=k_codes[0][:].bitcast(I32), in_=words[:, 0:KEY_LOAD])
         for quad in range(4):
-            nc.scalar.dma_start(out=k_scale[32 * quad : 32 * quad + 4, :].bitcast(I32), in_=scale_rows[4 * quad : 4 * quad + 4, :])
-
-        q_raw = sb.tile([P, PACK, Q], F32, name="q_raw")
-        nc.sync.dma_start(out=q_raw[:], in_=query.rearrange("(p j) q -> p j q", j=PACK))
-        words = keys_words[0].rearrange("p n t -> p (n t)").bitcast(I32)
-        k_codes = []
-        for c in range(T // KEY_LOAD):
-            t = sb.tile([P, KEY_LOAD], U32, name="k_codes%d" % c, align_bytes=64)
-            nc.sync.dma_start(out=t[:].bitcast(I32), in_=words[:, c * KEY_LOAD : (c + 1) * KEY_LOAD])
-            k_codes.append(t)
+            queue = nc.sync if quad < 2 else nc.scalar
+            queue.dma_start(
+                out=k_scale[32 * quad : 32 * quad + 16, :].bitcast(I32),
+                in_=scale_rows[4 * quad : 4 * quad + 4, :].rearrange("r (m c) -> m r c", m=4),
+            )
+        nc.sync.dma_start(out=k_codes[1][:].bitcast(I32), in_=words[:, KEY_LOAD:T])
         list2 = sb.tile([P, LIST_COLS], U16, name="list2")
         nc.sync.dma_start(list2[:], offs2)
         list1 = sb.tile([P, LIST_COLS], U16, name="list1")
         nc.sync.dma_start(list1[:], offs)
-        old_sb = sb.tile([P, T], F32, name="old_sb")
-        nc.sync.dma_start(out=old_sb[:], in_=old)
         list3 = sb.tile([P, LIST_COLS], U16, name="list3")
         nc.sync.dma_start(list3[:], offs3)
 
@@ -57,33 +60,37 @@ def tile_attend_difference_lean_throughtimes_heads_kernel(tc, query, keys_words,
         nc.vector.memset(f1[:], 0.0)
 
         q_bf = sb.tile([P, Q, PACK], BF16, name="q_bf", align_bytes=64)
-        nc.vector.tensor_copy(
-            out=q_bf[:].rearrange("p (c i) j -> p c j i", i=4),
-            in_=q_raw[:].rearrange("p j (c i) -> p c j i", i=4),
-        )
+        for u in range(2):
+            nc.vector.tensor_copy(
+                out=q_bf[:, :, 2 * u : 2 * u + 2].rearrange("p (c i) j -> p c j i", i=4),
+                in_=q_raw[u][:].rearrange("p j (c i) -> p c j i", i=4),
+            )
+        old_sb = sb.tile([P, T], F32, name="old_sb", tag="raw1")
+        nc.sync.dma_start(out=old_sb[:], in_=old)
         q_codes = sb.tile([P, Q], U32, name="q_codes", align_bytes=64)
         q_scale = sb.tile([P, Q], U8, name="q_scale", align_bytes=64)
         nc.vector.quantize_mx(out=q_codes[:].bitcast(FP8X4), scales=q_scale[:], in_=q_bf[:].rearrange("p q j -> p (q j)"))
 
         a = sb.tile([P, T], F32, name="a")
-        for m in range(T // N_MM):
-            t0 = m * N_MM
-            bank = ps.tile([P, N_MM], F32, name="bank%d" % m)
+        for n, (t0, width) in enumerate(PASSES):
+            bank = ps.tile([P, width], F32, name="bank%d" % n)
             codes = k_codes[t0 // KEY_LOAD]
             c0 = t0 % KEY_LOAD
+            m = t0 // N_MM
+            s0 = t0 % N_MM
             nc.tensor.matmul_mx(
                 out=bank[:],
                 lhsT=q_codes[:].bitcast(FP8X4),
                 lhsT_scale=q_scale[:],
-                rhs=codes[:, c0 : c0 + N_MM].bitcast(FP8X4),
-                rhs_scale=k_scale[:, t0 : t0 + N_MM],
+                rhs=codes[:, c0 : c0 + width].bitcast(FP8X4),
+                rhs_scale=k_scale[4 * m : P, s0 : s0 + width],
                 start=True,
                 stop=True,
             )
-            if m % 2 == 0:
-                nc.vector.tensor_copy(out=a[:, t0 : t0 + N_MM], in_=bank[:])
+            if n % 2 == 0:
+                nc.vector.tensor_copy(out=a[:, t0 : t0 + width], in_=bank[:])
             else:
-                nc.scalar.activation(a[:, t0 : t0 + N_MM], bank[:], COPY)
+                nc.scalar.activation(a[:, t0 : t0 + width], bank[:], COPY)
 
         def half(lst, h):
             return lst[:, h * LIST_COLS // 2 : (h + 1) * LIST_COLS // 2]
@@ -102,7 +109,8 @@ def tile_attend_difference_lean_throughtimes_heads_kernel(tc, query, keys_words,
 
         f2 = sb.tile([P, T], F32, name="f2")
         nc.vector.tensor_tensor(f2[:], f1[:], old_sb[:], ADD)
-        for h in range(2):
-            y = sb.tile([P, HALF], F32, name="y%d" % h)
-            nc.vector.tensor_tensor(y[:], f2[:].indirect(half(list3, h)), w[h][:], MULT)
-            nc.sync.dma_start(out=out[:, h * HALF : (h + 1) * HALF], in_=y[:])
+        for i0, width in PIECES:
+            y = sb.tile([P, width], F32, name="y%d" % i0)
+            w0 = i0 % HALF
+            nc.vector.tensor_tensor(y[:], f2[:].indirect(list3[:, i0 // 16 : (i0 + width) // 16]), w[i0 // HALF][:, w0 : w0 + width], MULT)
+            nc.sync.dma_start(out=out[:, i0 : i0 + width], in_=y[:])

@@ -22,6 +22,7 @@ LIST_COLS = I // 16
 KEY_LOAD = 512
 N_MM = 256
 HALF = I // 2
+Q_SPLIT = 64
 PASSES = ((0, 256), (256, 256), (512, 256), (768, 128), (896, 128))
 PIECES = ((0, 256), (256, 128), (384, 128))
 
@@ -43,8 +44,7 @@ def tile_attend_difference_lean_throughtimes_heads_kernel(tc, query, keys_words,
         scale_rows = keys_scales[0].bitcast(I32)
         nc.sync.dma_start(out=k_codes[0][:].bitcast(I32), in_=words[:, 0:KEY_LOAD])
         for quad in range(4):
-            queue = nc.sync if quad < 2 else nc.scalar
-            queue.dma_start(
+            nc.sync.dma_start(
                 out=k_scale[32 * quad : 32 * quad + 16, :].bitcast(I32),
                 in_=scale_rows[4 * quad : 4 * quad + 4, :].rearrange("r (m c) -> m r c", m=4),
             )
@@ -61,9 +61,15 @@ def tile_attend_difference_lean_throughtimes_heads_kernel(tc, query, keys_words,
 
         q_bf = sb.tile([P, Q, PACK], BF16, name="q_bf", align_bytes=64)
         for u in range(2):
+            dst = q_bf[:, :, 2 * u : 2 * u + 2]
             nc.vector.tensor_copy(
-                out=q_bf[:, :, 2 * u : 2 * u + 2].rearrange("p (c i) j -> p c j i", i=4),
-                in_=q_raw[u][:].rearrange("p j (c i) -> p c j i", i=4),
+                out=dst[:, 0:Q_SPLIT, :].rearrange("p (c i) j -> p c j i", i=4),
+                in_=q_raw[u][:, :, 0:Q_SPLIT].rearrange("p j (c i) -> p c j i", i=4),
+            )
+            nc.scalar.activation(
+                dst[:, Q_SPLIT:Q, :].rearrange("p (c i) j -> p c j i", i=4),
+                q_raw[u][:, :, Q_SPLIT:Q].rearrange("p j (c i) -> p c j i", i=4),
+                COPY,
             )
         old_sb = sb.tile([P, T], F32, name="old_sb", tag="raw1")
         nc.sync.dma_start(out=old_sb[:], in_=old)
@@ -98,8 +104,8 @@ def tile_attend_difference_lean_throughtimes_heads_kernel(tc, query, keys_words,
         plus = [sb.tile([P, HALF], F32, name="plus%d" % h) for h in range(2)]
         minus = [sb.tile([P, HALF], F32, name="minus%d" % h) for h in range(2)]
         w = [sb.tile([P, HALF], F32, name="w%d" % h) for h in range(2)]
-        nc.vector.tensor_scalar(minus[0][:], a[:].indirect(half(list2, 0)), -1.0, 0.0, MULT, ADD)
-        nc.scalar.activation(plus[0][:], a[:].indirect(half(list1, 0)), COPY)
+        nc.vector.tensor_copy(plus[0][:], a[:].indirect(half(list1, 0)))
+        nc.scalar.activation(minus[0][:], a[:].indirect(half(list2, 0)), COPY, scale=-1.0)
         nc.scalar.activation(plus[1][:], a[:].indirect(half(list1, 1)), COPY)
         nc.scalar.activation(minus[1][:], a[:].indirect(half(list2, 1)), COPY, scale=-1.0)
 
@@ -109,8 +115,12 @@ def tile_attend_difference_lean_throughtimes_heads_kernel(tc, query, keys_words,
 
         f2 = sb.tile([P, T], F32, name="f2")
         nc.vector.tensor_tensor(f2[:], f1[:], old_sb[:], ADD)
-        for i0, width in PIECES:
-            y = sb.tile([P, width], F32, name="y%d" % i0)
-            w0 = i0 % HALF
-            nc.vector.tensor_tensor(y[:], f2[:].indirect(list3[:, i0 // 16 : (i0 + width) // 16]), w[i0 // HALF][:, w0 : w0 + width], MULT)
-            nc.sync.dma_start(out=out[:, i0 : i0 + width], in_=y[:])
+        picked = sb.tile([P, HALF], F32, name="picked")
+        nc.scalar.activation(picked[:], f2[:].indirect(half(list3, 1)), COPY)
+        y0 = sb.tile([P, HALF], F32, name="y0")
+        nc.vector.tensor_tensor(y0[:], f2[:].indirect(half(list3, 0)), w[0][:], MULT)
+        nc.sync.dma_start(out=out[:, 0:HALF], in_=y0[:])
+        for c0 in range(0, HALF, P):
+            y1 = sb.tile([P, P], F32, name="y1_%d" % c0)
+            nc.vector.tensor_tensor(y1[:], picked[:, c0 : c0 + P], w[1][:, c0 : c0 + P], MULT)
+            nc.sync.dma_start(out=out[:, HALF + c0 : HALF + c0 + P], in_=y1[:])

@@ -22,7 +22,8 @@ LIST_COLS = I // 16
 KEY_LOAD = 512
 N_MM = 256
 HALF = I // 2
-Q_SPLIT = 64
+Q_SPLIT = 80
+KEY_LOADS = ((0, 512), (512, 256), (768, 256))
 PASSES = ((0, 256), (256, 256), (512, 256), (768, 128), (896, 128))
 PIECES = ((0, 256), (256, 128), (384, 128))
 
@@ -34,11 +35,10 @@ def tile_attend_difference_lean_throughtimes_heads_kernel(tc, query, keys_words,
         ps = ctx.enter_context(tc.psum_pool(name="ps", bufs=1))
 
         q_rows = query.rearrange("(p j) q -> p j q", j=PACK)
-        q_raw = [sb.tile([P, 2, Q], F32, name="q_raw%d" % u, tag="raw%d" % u) for u in range(2)]
-        for u in range(2):
-            nc.sync.dma_start(out=q_raw[u][:], in_=q_rows[:, 2 * u : 2 * u + 2, :])
+        q_raw = sb.tile([P, PACK, Q], F32, name="q_raw", tag="raw1")
+        nc.sync.dma_start(out=q_raw[:], in_=q_rows)
         words = keys_words[0].rearrange("p n t -> p (n t)").bitcast(I32)
-        k_codes = [sb.tile([P, KEY_LOAD], U32, name="k_codes%d" % c, align_bytes=64) for c in range(T // KEY_LOAD)]
+        k_codes = [sb.tile([P, width], U32, name="k_codes%d" % t0, align_bytes=64) for t0, width in KEY_LOADS]
         k_scale = sb.tile([P, N_MM], U8, name="k_scale", align_bytes=64)
         nc.vector.memset(k_scale[:].bitcast(I32), 0)
         scale_rows = keys_scales[0].bitcast(I32)
@@ -48,7 +48,9 @@ def tile_attend_difference_lean_throughtimes_heads_kernel(tc, query, keys_words,
                 out=k_scale[32 * quad : 32 * quad + 16, :].bitcast(I32),
                 in_=scale_rows[4 * quad : 4 * quad + 4, :].rearrange("r (m c) -> m r c", m=4),
             )
-        nc.sync.dma_start(out=k_codes[1][:].bitcast(I32), in_=words[:, KEY_LOAD:T])
+        for c in (1, 2):
+            t0, width = KEY_LOADS[c]
+            nc.sync.dma_start(out=k_codes[c][:].bitcast(I32), in_=words[:, t0 : t0 + width])
         list2 = sb.tile([P, LIST_COLS], U16, name="list2")
         nc.sync.dma_start(list2[:], offs2)
         list1 = sb.tile([P, LIST_COLS], U16, name="list1")
@@ -60,17 +62,15 @@ def tile_attend_difference_lean_throughtimes_heads_kernel(tc, query, keys_words,
         nc.vector.memset(f1[:], 0.0)
 
         q_bf = sb.tile([P, Q, PACK], BF16, name="q_bf", align_bytes=64)
-        for u in range(2):
-            dst = q_bf[:, :, 2 * u : 2 * u + 2]
-            nc.vector.tensor_copy(
-                out=dst[:, 0:Q_SPLIT, :].rearrange("p (c i) j -> p c j i", i=4),
-                in_=q_raw[u][:, :, 0:Q_SPLIT].rearrange("p j (c i) -> p c j i", i=4),
-            )
-            nc.scalar.activation(
-                dst[:, Q_SPLIT:Q, :].rearrange("p (c i) j -> p c j i", i=4),
-                q_raw[u][:, :, Q_SPLIT:Q].rearrange("p j (c i) -> p c j i", i=4),
-                COPY,
-            )
+        nc.vector.tensor_copy(
+            out=q_bf[:, 0:Q_SPLIT, :].rearrange("p (c i) j -> p c j i", i=4),
+            in_=q_raw[:, :, 0:Q_SPLIT].rearrange("p j (c i) -> p c j i", i=4),
+        )
+        nc.scalar.activation(
+            q_bf[:, Q_SPLIT:Q, :].rearrange("p (c i) j -> p c j i", i=4),
+            q_raw[:, :, Q_SPLIT:Q].rearrange("p j (c i) -> p c j i", i=4),
+            COPY,
+        )
         old_sb = sb.tile([P, T], F32, name="old_sb", tag="raw1")
         nc.sync.dma_start(out=old_sb[:], in_=old)
         q_codes = sb.tile([P, Q], U32, name="q_codes", align_bytes=64)
@@ -80,8 +80,9 @@ def tile_attend_difference_lean_throughtimes_heads_kernel(tc, query, keys_words,
         a = sb.tile([P, T], F32, name="a")
         for n, (t0, width) in enumerate(PASSES):
             bank = ps.tile([P, width], F32, name="bank%d" % n)
-            codes = k_codes[t0 // KEY_LOAD]
-            c0 = t0 % KEY_LOAD
+            c = max(j for j in range(3) if KEY_LOADS[j][0] <= t0)
+            codes = k_codes[c]
+            c0 = t0 - KEY_LOADS[c][0]
             m = t0 // N_MM
             s0 = t0 % N_MM
             nc.tensor.matmul_mx(

from contextlib import ExitStack

import concourse.mybir as mybir

D, T, I, Q = 512, 1024, 512, 128
FLOPS = 2 * D * Q * T

F32 = mybir.dt.float32
BF16 = mybir.dt.bfloat16
I32 = mybir.dt.int32
U32 = mybir.dt.uint32
U16 = mybir.dt.uint16
U8 = mybir.dt.uint8
FP8X4 = mybir.dt.float8_e4m3fn_x4
ADD = mybir.AluOpType.add
MULT = mybir.AluOpType.mult
COPY = mybir.ActivationFunctionType.Copy

P = 128
PACK = 4
LIST_COLS = I // 16
KEY_LOAD = 512
N_MM = 256
HALF = I // 2
Q_SPLIT = 80
KEY_LOADS = ((0, 512), (512, 256), (768, 256))
PASSES = ((0, 256), (256, 256), (512, 256), (768, 128), (896, 128))
PIECES = ((0, 256), (256, 128), (384, 128))


def tile_attend_difference_lean_throughtimes_heads_kernel(tc, query, keys_words, keys_scales, old, offs, offs2, offs3, out):
    nc = tc.nc
    with ExitStack() as ctx:
        sb = ctx.enter_context(tc.tile_pool(name="sb", bufs=1))
        ps = ctx.enter_context(tc.psum_pool(name="ps", bufs=1))

        q_rows = query.rearrange("(p j) q -> p j q", j=PACK)
        q_raw = sb.tile([P, PACK, Q], F32, name="q_raw", tag="raw1")
        nc.sync.dma_start(out=q_raw[:], in_=q_rows)
        words = keys_words[0].rearrange("p n t -> p (n t)").bitcast(I32)
        k_codes = [sb.tile([P, width], U32, name="k_codes%d" % t0, align_bytes=64) for t0, width in KEY_LOADS]
        k_scale = sb.tile([P, N_MM], U8, name="k_scale", align_bytes=64)
        nc.vector.memset(k_scale[:].bitcast(I32), 0)
        scale_rows = keys_scales[0].bitcast(I32)
        nc.sync.dma_start(out=k_codes[0][:].bitcast(I32), in_=words[:, 0:KEY_LOAD])
        for quad in range(4):
            nc.sync.dma_start(
                out=k_scale[32 * quad : 32 * quad + 16, :].bitcast(I32),
                in_=scale_rows[4 * quad : 4 * quad + 4, :].rearrange("r (m c) -> m r c", m=4),
            )
        for c in (1, 2):
            t0, width = KEY_LOADS[c]
            nc.sync.dma_start(out=k_codes[c][:].bitcast(I32), in_=words[:, t0 : t0 + width])
        list2 = sb.tile([P, LIST_COLS], U16, name="list2")
        nc.sync.dma_start(list2[:], offs2)
        list1 = sb.tile([P, LIST_COLS], U16, name="list1")
        nc.sync.dma_start(list1[:], offs)
        list3 = sb.tile([P, LIST_COLS], U16, name="list3")
        nc.sync.dma_start(list3[:], offs3)

        f1 = sb.tile([P, T], F32, name="f1")
        nc.vector.memset(f1[:], 0.0)

        q_bf = sb.tile([P, Q, PACK], BF16, name="q_bf", align_bytes=64)
        nc.vector.tensor_copy(
            out=q_bf[:, 0:Q_SPLIT, :].rearrange("p (c i) j -> p c j i", i=4),
            in_=q_raw[:, :, 0:Q_SPLIT].rearrange("p j (c i) -> p c j i", i=4),
        )
        nc.scalar.activation(
            q_bf[:, Q_SPLIT:Q, :].rearrange("p (c i) j -> p c j i", i=4),
            q_raw[:, :, Q_SPLIT:Q].rearrange("p j (c i) -> p c j i", i=4),
            COPY,
        )
        old_sb = sb.tile([P, T], F32, name="old_sb", tag="raw1")
        nc.sync.dma_start(out=old_sb[:], in_=old)
        q_codes = sb.tile([P, Q], U32, name="q_codes", align_bytes=64)
        q_scale = sb.tile([P, Q], U8, name="q_scale", align_bytes=64)
        nc.vector.quantize_mx(out=q_codes[:].bitcast(FP8X4), scales=q_scale[:], in_=q_bf[:].rearrange("p q j -> p (q j)"))

        a = sb.tile([P, T], F32, name="a")
        for n, (t0, width) in enumerate(PASSES):
            bank = ps.tile([P, width], F32, name="bank%d" % n)
            c = max(j for j in range(3) if KEY_LOADS[j][0] <= t0)
            codes = k_codes[c]
            c0 = t0 - KEY_LOADS[c][0]
            m = t0 // N_MM
            s0 = t0 % N_MM
            nc.tensor.matmul_mx(
                out=bank[:],
                lhsT=q_codes[:].bitcast(FP8X4),
                lhsT_scale=q_scale[:],
                rhs=codes[:, c0 : c0 + width].bitcast(FP8X4),
                rhs_scale=k_scale[4 * m : P, s0 : s0 + width],
                start=True,
                stop=True,
            )
            if n % 2 == 0:
                nc.vector.tensor_copy(out=a[:, t0 : t0 + width], in_=bank[:])
            else:
                nc.scalar.activation(a[:, t0 : t0 + width], bank[:], COPY)

        def half(lst, h):
            return lst[:, h * LIST_COLS // 2 : (h + 1) * LIST_COLS // 2]

        plus = [sb.tile([P, HALF], F32, name="plus%d" % h) for h in range(2)]
        minus = [sb.tile([P, HALF], F32, name="minus%d" % h) for h in range(2)]
        w = [sb.tile([P, HALF], F32, name="w%d" % h) for h in range(2)]
        nc.vector.tensor_copy(plus[0][:], a[:].indirect(half(list1, 0)))
        nc.scalar.activation(minus[0][:], a[:].indirect(half(list2, 0)), COPY, scale=-1.0)
        nc.scalar.activation(plus[1][:], a[:].indirect(half(list1, 1)), COPY)
        nc.scalar.activation(minus[1][:], a[:].indirect(half(list2, 1)), COPY, scale=-1.0)

        for h in range(2):
            nc.vector.tensor_tensor(f1[:].indirect(half(list1, h)), plus[h][:], minus[h][:], ADD)
            nc.vector.tensor_tensor(w[h][:], plus[h][:], minus[h][:], ADD)

        f2 = sb.tile([P, T], F32, name="f2")
        nc.vector.tensor_tensor(f2[:], f1[:], old_sb[:], ADD)
        picked = sb.tile([P, HALF], F32, name="picked")
        nc.scalar.activation(picked[:], f2[:].indirect(half(list3, 1)), COPY)
        y0 = sb.tile([P, HALF], F32, name="y0")
        nc.vector.tensor_tensor(y0[:], f2[:].indirect(half(list3, 0)), w[0][:], MULT)
        nc.sync.dma_start(out=out[:, 0:HALF], in_=y0[:])
        for c0 in range(0, HALF, P):
            y1 = sb.tile([P, P], F32, name="y1_%d" % c0)
            nc.vector.tensor_tensor(y1[:], picked[:, c0 : c0 + P], w[1][:, c0 : c0 + P], MULT)
            nc.sync.dma_start(out=out[:, HALF + c0 : HALF + c0 + P], in_=y1[:])
